import numpy as np
CORES = [2,10,18,26,34,42,50,58,66,74,82,90,98,106,114,122,130,138,146,154,162,170,178,186,194,202,210,218,226,234,242,250]
N = 32
COUNTS = [[0,0,0,0,1,0,1,1,0,1,1,1,0,1,1,1,4,0,1,1,0,1,0,1,1,1,0,0,1,0,1,1],[0,0,1,0,1,1,1,0,1,1,1,0,0,1,0,0,4,1,0,1,1,1,0,1,1,0,1,1,0,0,0,0],[1,1,0,1,1,1,1,1,1,1,0,0,0,1,1,1,4,1,0,1,1,0,1,0,0,1,0,0,1,0,1,1],[1,1,1,0,1,1,1,1,1,1,0,0,1,1,1,1,4,1,1,1,1,1,1,1,1,0,0,1,0,1,0,0],[0,1,1,0,0,1,1,1,1,1,0,0,1,0,1,1,4,1,1,1,0,0,0,1,0,1,1,1,1,1,1,1],[1,1,0,0,0,0,1,1,1,0,1,1,0,0,1,0,4,1,1,1,1,1,1,1,1,0,0,1,1,0,0,1],[0,1,1,0,0,0,0,0,1,0,1,1,0,0,0,0,4,1,1,0,1,0,1,0,0,1,1,0,0,0,0,0],[0,0,1,1,1,0,1,0,0,0,1,1,1,1,1,0,4,1,0,1,1,0,0,1,1,1,1,1,0,0,1,1],[0,0,1,1,0,1,1,1,0,1,1,1,0,1,0,1,4,0,0,1,0,0,1,1,0,1,0,0,1,1,1,1],[1,1,1,0,1,1,0,1,0,0,1,1,1,1,1,0,4,1,0,0,1,0,0,1,0,1,1,1,1,0,1,1],[1,1,0,0,1,0,1,1,1,1,0,0,1,0,0,1,4,0,1,1,1,0,1,0,0,0,1,1,0,1,0,0],[1,1,1,0,1,1,0,1,1,1,1,0,1,0,1,1,4,0,1,0,1,1,1,1,1,1,1,0,1,1,1,0],[0,0,1,1,1,1,1,1,1,0,1,0,0,1,1,0,4,0,1,0,1,1,0,1,1,1,1,0,1,0,1,1],[1,1,1,0,1,1,0,1,1,1,1,1,1,0,1,1,4,1,1,1,1,0,1,1,1,1,0,1,1,0,1,1],[1,0,1,0,1,1,1,1,0,1,0,0,1,0,0,1,4,1,1,1,1,1,0,0,1,0,0,1,0,1,1,0],[0,1,1,0,0,1,1,1,1,0,0,1,0,1,1,0,4,1,0,1,1,1,0,1,0,1,1,1,1,0,0,0],[0,1,1,1,0,1,0,1,0,0,1,0,1,1,1,1,0,0,1,1,1,1,1,0,0,1,0,1,0,0,0,1],[1,1,1,0,1,1,1,1,1,1,0,1,1,1,1,1,4,0,1,0,0,1,1,0,1,1,0,0,1,1,1,1],[1,0,1,1,1,1,1,0,1,0,1,0,0,1,1,0,4,1,0,1,0,0,1,1,1,0,1,0,1,1,0,0],[1,1,0,1,0,1,0,0,1,1,0,0,1,1,0,1,4,1,1,0,1,0,1,0,1,1,1,0,0,1,1,1],[1,1,1,1,1,1,1,0,0,1,1,1,1,1,1,0,4,0,1,1,0,1,0,1,1,1,0,1,1,1,1,1],[1,1,1,1,0,1,0,1,0,1,1,1,0,1,1,1,4,0,1,0,1,0,1,0,1,1,1,1,0,1,1,0],[1,0,0,1,1,0,1,1,1,1,0,1,0,1,1,1,4,1,1,1,1,1,0,0,1,1,1,0,1,1,1,0],[0,1,1,1,1,1,1,1,1,1,0,1,1,0,1,0,4,1,1,1,1,0,0,0,0,1,0,1,1,0,1,0],[1,1,0,1,1,0,0,0,0,1,1,1,1,1,0,0,4,1,0,1,1,1,1,1,0,0,1,1,1,1,0,1],[1,1,1,0,0,1,1,1,0,0,1,1,0,1,1,0,4,1,0,1,1,1,1,0,0,0,1,1,1,1,1,1],[1,1,1,1,1,0,1,1,0,1,0,1,1,1,1,1,4,1,1,0,1,1,1,1,1,1,0,1,1,1,1,0],[1,1,0,1,1,1,1,1,1,0,1,0,0,1,1,0,4,1,1,0,1,1,1,0,1,0,1,0,0,0,1,1],[1,1,1,1,0,0,0,1,1,1,1,1,0,1,0,1,4,1,1,1,1,0,1,1,0,1,1,1,0,1,1,0],[1,0,1,1,1,1,1,0,1,1,1,1,0,1,0,0,4,1,0,1,1,1,0,1,1,1,0,0,1,0,1,1],[1,0,0,1,1,1,1,1,0,1,0,1,0,1,1,0,4,0,0,1,1,1,1,0,1,0,1,1,1,0,0,1],[1,1,0,1,0,1,0,0,0,1,0,1,1,1,1,0,4,0,1,0,0,1,1,0,0,1,1,1,1,0,0,0]]
XW, YW = 29, 124
def setup_inputs(rng):
    return {"x": rng.standard_normal((N, 128, XW), dtype=np.float32)}
def reference(x):
    y = np.full((N, 128, YW), np.nan, x.dtype)
    fill = [0] * N
    for s in range(N):
        o = 0
        for d in range(N):
            c = COUNTS[s][d]
            y[d][:, fill[d]:fill[d] + c] = x[s][:, o:o + c]
            o += c; fill[d] += c
    return {"y": y}

@@ -1,0 +1,167 @@
+from concourse.bass import DstId, RemoteDMATransfer
+
+FEED = "sbuf"
+RANK_EXTRA = 2
+XW, YW = 29, 124
+
+SCRATCH = {
+    "xs": ("sbuf", [128, XW], "float32"),
+    "land": ("sbuf", [128, YW], "float32"),
+}
+if FEED == "dram":
+    SCRATCH["xd"] = ("dram", [128, XW], "float32")
+SEMAPHORES = ["loaded", "copied", "fed", "arrived", "sent", "stored"]
+
+MASKS = {1: [0xFF], 2: [0x0F, 0xF0], 4: [0x03, 0x0C, 0x30, 0xC0]}
+CACHE = {}
+
+
+def bits(m):
+    return bin(m).count("1")
+
+
+def call_sizes(m):
+    out = []
+    while m >= 4:
+        out.append(4)
+        m -= 4
+    if m == 3:
+        out += [2, 1]
+    elif m:
+        out.append(m)
+    return out
+
+
+def calls_of(jobs):
+    calls = []
+    for w in sorted(set(j[1] for j in jobs), reverse=True):
+        group = [j for j in jobs if j[1] == w]
+        i = 0
+        for n in call_sizes(len(group)):
+            calls.append([(group[i + k], MASKS[n][k]) for k in range(n)])
+            i += n
+    return calls
+
+
+def plan(T, topo):
+    if "p" in CACHE:
+        return CACHE["p"]
+    counts, cores = T.tables["COUNTS"], list(T.cores)
+    n = len(cores)
+    jobs, feeds, owner = {}, {}, {}
+    arrive = [0] * n
+    for s in range(n):
+        rc = cores[s]
+        base = rc - rc % 8
+        chipc = [base + i for i in range(8)]
+        for c in chipc:
+            owner[c] = s
+            jobs[c] = []
+        load = dict((c, 0) for c in chipc)
+        load[rc] = -RANK_EXTRA
+        items = []
+        xo = 0
+        for d in range(n):
+            w = counts[s][d]
+            if w and d != s:
+                items.append((d, w, xo, sum(counts[q][d] for q in range(s))))
+            xo += w
+        die = (s >> 1) & 1
+
+        def place(it, cands):
+            c = min(cands, key=lambda c: (load[c], c == rc, c))
+            jobs[c].append(it)
+            load[c] += 1
+
+        wide = [it for it in items if it[1] > 1]
+        thin = [it for it in items if it[1] == 1]
+        for it in wide:
+            ok = [c for c in chipc if topo.may_write(c, cores[it[0]]) and c != rc]
+            place(it, [c for c in ok if topo.die(c) == die] or ok)
+        hard = [it for it in thin if not all(topo.may_write(c, cores[it[0]]) for c in chipc)]
+        easy = [it for it in thin if it not in hard]
+        for it in hard + easy:
+            place(it, [c for c in chipc if topo.may_write(c, cores[it[0]])])
+        feeds[s] = sorted([c for c in chipc if c != rc and jobs[c]], key=lambda c: (-len(jobs[c]), c))
+        for c in chipc:
+            for call in calls_of(jobs[c]):
+                for it, m in call:
+                    arrive[it[0]] += bits(m)
+    CACHE["p"] = (jobs, feeds, owner, arrive)
+    return CACHE["p"]
+
+
+def send(g, core, T, topo, jobs):
+    total = 0
+    for call in calls_of(jobs):
+        trs = []
+        for (d, w, xo, yo), m in call:
+            rid, pid = topo.addr(T.cores[d], core)
+            total += bits(m)
+            if len(call) == 1:
+                g.remote_dma(out_ap=T.land[:, yo:yo + w], in_ap=T.xs[:, xo:xo + w], remote_sem=T.sem.arrived,
+                             local_sem=T.sem.sent, pid=pid, routing_id=rid, dma_engine_mask=m)
+            else:
+                trs.append(RemoteDMATransfer(dst_ids=[DstId(rid=rid, pnc=pid)], dma_engine_mask=m,
+                                             remote_sem=T.sem.arrived, src=T.xs[:, xo:xo + w],
+                                             dst=T.land[:, yo:yo + w]))
+        if trs:
+            g.remote_dma_fused(trs, local_sem=T.sem.sent)
+    return total
+
+
+def rank_program(g, core, T, topo):
+    jobs, feeds, owner, arrive = plan(T, topo)
+    if core not in owner:
+        return
+    rank = T.rank_of(core)
+    s = owner[core]
+    if rank is None:
+        if not jobs[core]:
+            return
+        if FEED == "dram":
+            g.sync.wait_ge(T.sem.fed, 16)
+            g.sync.dma_start(T.xs[:], T.xd[:]).then_inc(T.sem.loaded, 16)
+            g.wait_ge(T.sem.loaded, 16)
+        else:
+            g.wait_ge(T.sem.fed, 16)
+        g.wait_ge(T.sem.sent, send(g, core, T, topo, jobs[core]))
+        return
+
+    counts = T.tables["COUNTS"]
+    width = sum(counts[q][rank] for q in range(len(T.cores)))
+    ids = []
+    for h in feeds[s]:
+        rid, pid = topo.addr(h, core)
+        ids.append(DstId(rid=rid, pnc=pid))
+    sent = 0
+    if FEED == "dram":
+        g.sync.dma_start(T.xd[:], T.x[:]).then_inc(T.sem.copied, 16)
+        g.scalar.dma_start(T.xs[:], T.x[:]).then_inc(T.sem.loaded, 16)
+        if ids:
+            g.wait_ge(T.sem.copied, 16)
+            g.remote_dma_fused([RemoteDMATransfer(dst_ids=ids, dma_engine_mask=0xFFFF, remote_sem=T.sem.fed,
+                                                  srcs=[T.xd[:]], dsts=[T.xd[:] for h in ids])], local_sem=T.sem.sent)
+            sent += 16
+        else:
+            g.wait_ge(T.sem.copied, 16)
+        g.wait_ge(T.sem.loaded, 16)
+    else:
+        g.sync.dma_start(T.xs[:], T.x[:]).then_inc(T.sem.loaded, 16)
+        g.wait_ge(T.sem.loaded, 16)
+        if ids:
+            g.remote_dma_fused([RemoteDMATransfer(dst_ids=ids, dma_engine_mask=0xFFFF, remote_sem=T.sem.fed,
+                                                  srcs=[T.xs[:]], dsts=[T.xs[:] for h in ids])], local_sem=T.sem.sent)
+            sent += 16
+    sent += send(g, core, T, topo, jobs[core])
+
+    own = counts[rank][rank]
+    if own:
+        xo = sum(counts[rank][:rank])
+        yo = sum(counts[q][rank] for q in range(rank))
+        g.scalar.wait_ge(T.sem.loaded, 16)
+        g.scalar.dma_start(T.land[:, yo:yo + own], T.xs[:, xo:xo + own]).then_inc(T.sem.arrived, 16)
+    g.sync.wait_ge(T.sem.arrived, arrive[rank] + (16 if own else 0))
+    g.sync.dma_start(T.y[:, 0:width], T.land[:, 0:width]).then_inc(T.sem.stored, 16)
+    g.wait_ge(T.sem.sent, sent)
+    g.wait_ge(T.sem.stored, 16)

@@ -1,16 +1,15 @@
 from concourse.bass import DstId, RemoteDMATransfer
 
-FEED = "sbuf"
-RANK_EXTRA = 2
+STEP = 0.45
+HELP_OFF = 1.5
+RANK_OFF = 3.15
 XW, YW = 29, 124
 
 SCRATCH = {
     "xs": ("sbuf", [128, XW], "float32"),
     "land": ("sbuf", [128, YW], "float32"),
 }
-if FEED == "dram":
-    SCRATCH["xd"] = ("dram", [128, XW], "float32")
-SEMAPHORES = ["loaded", "copied", "fed", "arrived", "sent", "stored"]
+SEMAPHORES = ["loaded", "fed", "arrived", "sent", "stored"]
 
 MASKS = {1: [0xFF], 2: [0x0F, 0xF0], 4: [0x03, 0x0C, 0x30, 0xC0]}
 CACHE = {}
@@ -57,8 +56,6 @@ def plan(T, topo):
         for c in chipc:
             owner[c] = s
             jobs[c] = []
-        load = dict((c, 0) for c in chipc)
-        load[rc] = -RANK_EXTRA
         items = []
         xo = 0
         for d in range(n):
@@ -67,22 +64,30 @@ def plan(T, topo):
                 items.append((d, w, xo, sum(counts[q][d] for q in range(s))))
             xo += w
         die = (s >> 1) & 1
-
-        def place(it, cands):
-            c = min(cands, key=lambda c: (load[c], c == rc, c))
-            jobs[c].append(it)
-            load[c] += 1
-
         wide = [it for it in items if it[1] > 1]
         thin = [it for it in items if it[1] == 1]
+        port = [c for c in chipc if c != rc and all(topo.may_write(c, cores[d]) for d in range(n) if d != s)]
+        noport = [c for c in chipc if c != rc and c not in port]
+        order = []
         for it in wide:
-            ok = [c for c in chipc if topo.may_write(c, cores[it[0]]) and c != rc]
-            place(it, [c for c in ok if topo.die(c) == die] or ok)
+            ok = [c for c in port + noport if topo.may_write(c, cores[it[0]]) and c not in order]
+            order.append(([c for c in ok if topo.die(c) == die] or ok)[0])
+            jobs[order[-1]].append(it)
+        a, b = [c for c in port if c not in order], [c for c in noport if c not in order]
+        while a or b:
+            if a:
+                order.append(a.pop(0))
+            if b:
+                order.append(b.pop(0))
+        load = dict((c, HELP_OFF + STEP * (i + 1) + len(jobs[c])) for i, c in enumerate(order))
+        load[rc] = RANK_OFF
         hard = [it for it in thin if not all(topo.may_write(c, cores[it[0]]) for c in chipc)]
         easy = [it for it in thin if it not in hard]
         for it in hard + easy:
-            place(it, [c for c in chipc if topo.may_write(c, cores[it[0]])])
-        feeds[s] = sorted([c for c in chipc if c != rc and jobs[c]], key=lambda c: (-len(jobs[c]), c))
+            c = min([c for c in chipc if topo.may_write(c, cores[it[0]])], key=lambda c: (load[c], c))
+            jobs[c].append(it)
+            load[c] += 1
+        feeds[s] = [c for c in order if jobs[c]]
         for c in chipc:
             for call in calls_of(jobs[c]):
                 for it, m in call:
@@ -117,15 +122,9 @@ def rank_program(g, core, T, topo):
     rank = T.rank_of(core)
     s = owner[core]
     if rank is None:
-        if not jobs[core]:
-            return
-        if FEED == "dram":
-            g.sync.wait_ge(T.sem.fed, 16)
-            g.sync.dma_start(T.xs[:], T.xd[:]).then_inc(T.sem.loaded, 16)
-            g.wait_ge(T.sem.loaded, 16)
-        else:
+        if jobs[core]:
             g.wait_ge(T.sem.fed, 16)
-        g.wait_ge(T.sem.sent, send(g, core, T, topo, jobs[core]))
+            g.wait_ge(T.sem.sent, send(g, core, T, topo, jobs[core]))
         return
 
     counts = T.tables["COUNTS"]
@@ -135,24 +134,12 @@ def rank_program(g, core, T, topo):
         rid, pid = topo.addr(h, core)
         ids.append(DstId(rid=rid, pnc=pid))
     sent = 0
-    if FEED == "dram":
-        g.sync.dma_start(T.xd[:], T.x[:]).then_inc(T.sem.copied, 16)
-        g.scalar.dma_start(T.xs[:], T.x[:]).then_inc(T.sem.loaded, 16)
-        if ids:
-            g.wait_ge(T.sem.copied, 16)
-            g.remote_dma_fused([RemoteDMATransfer(dst_ids=ids, dma_engine_mask=0xFFFF, remote_sem=T.sem.fed,
-                                                  srcs=[T.xd[:]], dsts=[T.xd[:] for h in ids])], local_sem=T.sem.sent)
-            sent += 16
-        else:
-            g.wait_ge(T.sem.copied, 16)
-        g.wait_ge(T.sem.loaded, 16)
-    else:
-        g.sync.dma_start(T.xs[:], T.x[:]).then_inc(T.sem.loaded, 16)
-        g.wait_ge(T.sem.loaded, 16)
-        if ids:
-            g.remote_dma_fused([RemoteDMATransfer(dst_ids=ids, dma_engine_mask=0xFFFF, remote_sem=T.sem.fed,
-                                                  srcs=[T.xs[:]], dsts=[T.xs[:] for h in ids])], local_sem=T.sem.sent)
-            sent += 16
+    g.sync.dma_start(T.xs[:], T.x[:]).then_inc(T.sem.loaded, 16)
+    g.wait_ge(T.sem.loaded, 16)
+    if ids:
+        g.remote_dma_fused([RemoteDMATransfer(dst_ids=ids, dma_engine_mask=0xFFFF, remote_sem=T.sem.fed,
+                                              srcs=[T.xs[:]], dsts=[T.xs[:] for h in ids])], local_sem=T.sem.sent)
+        sent += 16
     sent += send(g, core, T, topo, jobs[core])
 
     own = counts[rank][rank]

from concourse.bass import DstId, RemoteDMATransfer

STEP = 0.45
HELP_OFF = 1.5
RANK_OFF = 3.15
XW, YW = 29, 124

SCRATCH = {
    "xs": ("sbuf", [128, XW], "float32"),
    "land": ("sbuf", [128, YW], "float32"),
}
SEMAPHORES = ["loaded", "fed", "arrived", "sent", "stored"]

MASKS = {1: [0xFF], 2: [0x0F, 0xF0], 4: [0x03, 0x0C, 0x30, 0xC0]}
CACHE = {}


def bits(m):
    return bin(m).count("1")


def call_sizes(m):
    out = []
    while m >= 4:
        out.append(4)
        m -= 4
    if m == 3:
        out += [2, 1]
    elif m:
        out.append(m)
    return out


def calls_of(jobs):
    calls = []
    for w in sorted(set(j[1] for j in jobs), reverse=True):
        group = [j for j in jobs if j[1] == w]
        i = 0
        for n in call_sizes(len(group)):
            calls.append([(group[i + k], MASKS[n][k]) for k in range(n)])
            i += n
    return calls


def plan(T, topo):
    if "p" in CACHE:
        return CACHE["p"]
    counts, cores = T.tables["COUNTS"], list(T.cores)
    n = len(cores)
    jobs, feeds, owner = {}, {}, {}
    arrive = [0] * n
    for s in range(n):
        rc = cores[s]
        base = rc - rc % 8
        chipc = [base + i for i in range(8)]
        for c in chipc:
            owner[c] = s
            jobs[c] = []
        items = []
        xo = 0
        for d in range(n):
            w = counts[s][d]
            if w and d != s:
                items.append((d, w, xo, sum(counts[q][d] for q in range(s))))
            xo += w
        die = (s >> 1) & 1
        wide = [it for it in items if it[1] > 1]
        thin = [it for it in items if it[1] == 1]
        port = [c for c in chipc if c != rc and all(topo.may_write(c, cores[d]) for d in range(n) if d != s)]
        noport = [c for c in chipc if c != rc and c not in port]
        order = []
        for it in wide:
            ok = [c for c in port + noport if topo.may_write(c, cores[it[0]]) and c not in order]
            order.append(([c for c in ok if topo.die(c) == die] or ok)[0])
            jobs[order[-1]].append(it)
        a, b = [c for c in port if c not in order], [c for c in noport if c not in order]
        while a or b:
            if a:
                order.append(a.pop(0))
            if b:
                order.append(b.pop(0))
        load = dict((c, HELP_OFF + STEP * (i + 1) + len(jobs[c])) for i, c in enumerate(order))
        load[rc] = RANK_OFF
        hard = [it for it in thin if not all(topo.may_write(c, cores[it[0]]) for c in chipc)]
        easy = [it for it in thin if it not in hard]
        for it in hard + easy:
            c = min([c for c in chipc if topo.may_write(c, cores[it[0]])], key=lambda c: (load[c], c))
            jobs[c].append(it)
            load[c] += 1
        feeds[s] = [c for c in order if jobs[c]]
        for c in chipc:
            for call in calls_of(jobs[c]):
                for it, m in call:
                    arrive[it[0]] += bits(m)
    CACHE["p"] = (jobs, feeds, owner, arrive)
    return CACHE["p"]


def send(g, core, T, topo, jobs):
    total = 0
    for call in calls_of(jobs):
        trs = []
        for (d, w, xo, yo), m in call:
            rid, pid = topo.addr(T.cores[d], core)
            total += bits(m)
            if len(call) == 1:
                g.remote_dma(out_ap=T.land[:, yo:yo + w], in_ap=T.xs[:, xo:xo + w], remote_sem=T.sem.arrived,
                             local_sem=T.sem.sent, pid=pid, routing_id=rid, dma_engine_mask=m)
            else:
                trs.append(RemoteDMATransfer(dst_ids=[DstId(rid=rid, pnc=pid)], dma_engine_mask=m,
                                             remote_sem=T.sem.arrived, src=T.xs[:, xo:xo + w],
                                             dst=T.land[:, yo:yo + w]))
        if trs:
            g.remote_dma_fused(trs, local_sem=T.sem.sent)
    return total


def rank_program(g, core, T, topo):
    jobs, feeds, owner, arrive = plan(T, topo)
    if core not in owner:
        return
    rank = T.rank_of(core)
    s = owner[core]
    if rank is None:
        if jobs[core]:
            g.wait_ge(T.sem.fed, 16)
            g.wait_ge(T.sem.sent, send(g, core, T, topo, jobs[core]))
        return

    counts = T.tables["COUNTS"]
    width = sum(counts[q][rank] for q in range(len(T.cores)))
    ids = []
    for h in feeds[s]:
        rid, pid = topo.addr(h, core)
        ids.append(DstId(rid=rid, pnc=pid))
    sent = 0
    g.sync.dma_start(T.xs[:], T.x[:]).then_inc(T.sem.loaded, 16)
    g.wait_ge(T.sem.loaded, 16)
    if ids:
        g.remote_dma_fused([RemoteDMATransfer(dst_ids=ids, dma_engine_mask=0xFFFF, remote_sem=T.sem.fed,
                                              srcs=[T.xs[:]], dsts=[T.xs[:] for h in ids])], local_sem=T.sem.sent)
        sent += 16
    sent += send(g, core, T, topo, jobs[core])

    own = counts[rank][rank]
    if own:
        xo = sum(counts[rank][:rank])
        yo = sum(counts[q][rank] for q in range(rank))
        g.scalar.wait_ge(T.sem.loaded, 16)
        g.scalar.dma_start(T.land[:, yo:yo + own], T.xs[:, xo:xo + own]).then_inc(T.sem.arrived, 16)
    g.sync.wait_ge(T.sem.arrived, arrive[rank] + (16 if own else 0))
    g.sync.dma_start(T.y[:, 0:width], T.land[:, 0:width]).then_inc(T.sem.stored, 16)
    g.wait_ge(T.sem.sent, sent)
    g.wait_ge(T.sem.stored, 16)
